import numpy as np
import ml_dtypes


def mxq(x, axis, fmt="e4m3"):
    dtype, down = {"e4m3": (ml_dtypes.float8_e4m3fn, 7), "e5m2": (ml_dtypes.float8_e5m2, 14)}[fmt]
    v = np.moveaxis(np.asarray(x, np.float32).astype(ml_dtypes.bfloat16).astype(np.float64), axis, -1)
    blocks = v.reshape(v.shape[:-1] + (-1, 32))
    amax = np.abs(blocks).max(-1, keepdims=True)
    byte = np.maximum(np.where(amax > 0, np.frexp(amax)[1] - 1 + 127, 0) - down, 1)
    scale = np.exp2(byte - 127.0)
    codes = (blocks / scale).astype(np.float32).astype(dtype).astype(np.float64)
    return np.moveaxis((codes * scale).reshape(v.shape), -1, axis)


WIDE = False


def mx_kscale(k):
    if not WIDE:
        return np.ones(k)
    levels = np.array([10, -10, 5, -5, 0])
    if k % 512:
        return np.exp2(np.random.permutation(np.resize(levels, k // 32))).repeat(32)
    a = np.empty((k // 512, 16))
    for p in range(k // 512):
        a[p, :8] = np.random.permutation(np.resize(levels, 8))
        for g in range(8):
            far = levels[np.abs(levels - a[p, g]) >= 10]
            a[p, g + 8] = far[np.random.randint(len(far))]
    return np.exp2(a.ravel()).repeat(32)


def f64(x):
    return np.asarray(x).astype(np.float64)


def striped8(idx):
    return np.asarray(idx).reshape(8, -1, 16).transpose(0, 2, 1).reshape(128, -1).astype(np.uint16)


def unstriped8(offs):
    return offs.reshape(8, 16, -1).transpose(0, 2, 1).reshape(8, -1).astype(np.int64)


def pick8(x, idx, run):
    r = np.arange(len(x))
    return x[r[:, None], idx[r % (8 * run) // run]]


E2M1 = np.array([0.0, 0.5, 1.0, 1.5, 2.0, 3.0, 4.0, 6.0, -0.0, -0.5, -1.0, -1.5, -2.0, -3.0, -4.0, -6.0])


def pack_weight(w, fmt):
    k, n = w.shape
    w = f64(np.asarray(w, np.float32).astype(ml_dtypes.bfloat16)).reshape(k // 32, 32, n)
    amax = np.abs(w).max(1)
    if fmt == "e4m3":
        byte = np.frexp(amax)[1] - 1 + 127 - 7
    else:
        mant, ex = np.frexp(amax / 6.0)
        byte = np.where(mant > 0.5, ex, ex - 1) + 127
    byte = np.clip(np.where(amax > 0, byte, 1), 1, 254)
    scaled = (w * np.exp2(127.0 - byte)[:, None, :]).reshape(k, n).astype(np.float32)
    by_word = np.ascontiguousarray(scaled.reshape(k // 512, 128, 4, n).transpose(0, 1, 3, 2))
    if fmt == "e4m3":
        words = by_word.astype(ml_dtypes.float8_e4m3fn).view(np.uint8)
    else:
        c = by_word.astype(ml_dtypes.float4_e2m1fn).view(np.uint8) & 0xF
        words = (c[..., 0::2] | (c[..., 1::2] << 4)).reshape(k // 512, 128, 2 * n)
    return np.ascontiguousarray(words), np.ascontiguousarray(byte.astype(np.uint8).reshape(k // 512, 16, n))


def unpack_weight(words, scales, fmt):
    g, _, n = scales.shape
    words = np.ascontiguousarray(words).reshape(g, 128, n, -1)
    if fmt == "e4m3":
        vals = words.view(ml_dtypes.float8_e4m3fn).astype(np.float64)
    else:
        nib = np.empty((g, 128, n, 4), np.uint8)
        nib[..., 0::2] = words & 0xF
        nib[..., 1::2] = words >> 4
        vals = E2M1[nib]
    vals = vals * np.repeat(np.exp2(scales.astype(np.float64) - 127.0), 8, axis=1)[..., None]
    return vals.transpose(0, 1, 3, 2).reshape(g * 512, n)


D, T, I, Q, G = 512, 1024, 512, 128, 64


def setup_inputs():
    n = np.random.standard_normal
    idx = np.stack([np.random.permutation(T)[:I] for _ in range(8)])
    idx2 = np.stack([np.random.permutation(T)[:I] for _ in range(8)])
    idx3 = np.stack([np.random.permutation(T)[:I] for _ in range(8)])
    fd = mx_kscale(D)
    keysp = pack_weight(n((D, T)) / fd[:, None], "e2m1")
    return {
        "query": (n((D, Q)) * 1.2 / np.sqrt(D) * fd[:, None]).astype(np.float32),
        "keys_words": keysp[0],
        "keys_scales": keysp[1],
        "lam": (np.random.uniform(0.2, 0.7, (Q, 1))).astype(np.float32),
        "base": (0.3 * n((Q, I))).astype(np.float32),
        "gain2": (np.random.uniform(0.5, 2.0, (Q, 1))).astype(np.float32),
        "offs": striped8(idx),
        "offs2": striped8(idx2),
        "offs3": striped8(idx3),
    }


def reference(query, keys_words, keys_scales, lam, base, gain2, offs, offs2, offs3):
    idx = unstriped8(offs)
    idx2 = unstriped8(offs2)
    idx3 = unstriped8(offs3)
    keysu = unpack_weight(keys_words, keys_scales, "e2m1")
    queryq = mxq(f64(query), 0, "e4m3")
    a = queryq.T @ keysu
    mx3 = np.maximum(np.maximum(pick8(a, idx, 16), pick8(a, idx2, 16)), pick8(a, idx3, 16))
    mn3 = np.minimum(np.minimum(pick8(a, idx, 16), pick8(a, idx2, 16)), pick8(a, idx3, 16))
    s = (pick8(a, idx, 16) + pick8(a, idx2, 16) + pick8(a, idx3, 16)) / 3.0 - (mx3 - mn3) * f64(lam)
    bm = s.reshape(Q, G, I // G).max(axis=2)
    bmr = np.repeat(bm, I // G, axis=1)
    p = np.exp(s - bmr)
    pg = p.reshape(Q, G, I // G).sum(axis=2)
    eg = np.exp(bm - np.max(bm, axis=1, keepdims=True))
    k0 = eg / np.sum(eg, axis=1, keepdims=True) / pg
    kr = np.repeat(k0, I // G, axis=1)
    w = p * kr
    y = np.tanh(w * f64(gain2) * 128.0) + f64(base)
    return y

@@ -1,0 +1,166 @@
+from contextlib import ExitStack
+
+import concourse.mybir as mybir
+
+D, T, I, Q, G = 512, 1024, 512, 128, 64
+FLOPS = 2 * D * T * Q
+
+F32 = mybir.dt.float32
+BF16 = mybir.dt.bfloat16
+I32 = mybir.dt.int32
+U32 = mybir.dt.uint32
+U16 = mybir.dt.uint16
+U8 = mybir.dt.uint8
+FP8X4 = mybir.dt.float8_e4m3fn_x4
+FP4X4 = mybir.dt.float4_e2m1fn_x4
+ALU = mybir.AluOpType
+ACT = mybir.ActivationFunctionType
+AX = mybir.AxisListType
+
+P = 128
+RUN = I // G
+N_MM = 256
+CHUNK = 256
+CHUNKS = I // CHUNK
+RUNS = CHUNK // RUN
+BIG = 1e30
+
+
+def tile_attend_spreadof3_bestofruns_gated_heads_kernel(
+    tc, query, keys_words, keys_scales, lam, base, gain2, offs, offs2, offs3, out
+):
+    nc = tc.nc
+    with ExitStack() as ctx:
+        keep = ctx.enter_context(tc.tile_pool(name="keep", bufs=1))
+        psum = ctx.enter_context(tc.psum_pool(name="psum", bufs=1))
+
+        k_scales = keep.tile([P, T], U8, align_bytes=64, name="k_scales")
+        nc.vector.memset(k_scales[:].bitcast(I32), 0)
+
+        q_raw = keep.tile([P, 4, Q], F32, name="q_raw", tag="rows")
+        nc.sync.dma_start(out=q_raw[:], in_=query.rearrange("(p j) q -> p j q", j=4))
+        k_words = keep.tile([P, 2 * T], U8, align_bytes=64, name="k_words")
+        nc.sync.dma_start(out=k_words[:].bitcast(I32), in_=keys_words[0].bitcast(I32))
+        for r in range(4):
+            nc.scalar.dma_start(
+                out=k_scales[r:P:32, :].bitcast(I32), in_=keys_scales[0][r:16:4, :].bitcast(I32)
+            )
+        lists = []
+        for n, src in enumerate((offs, offs2, offs3)):
+            tile = keep.tile([P, I // 16], U16, name="list%d" % n)
+            nc.sync.dma_start(tile[:], src)
+            lists.append(tile)
+        lam_col = keep.tile([P, 1], F32, name="lam_col")
+        nc.gpsimd.dma_start(out=lam_col[:], in_=lam)
+        gain_col = keep.tile([P, 1], F32, name="gain_col")
+        nc.gpsimd.dma_start(out=gain_col[:], in_=gain2)
+
+        q_bf = keep.tile([P, Q, 4], BF16, align_bytes=64, name="q_bf")
+        nc.vector.tensor_copy(
+            out=q_bf[:].rearrange("p (c i) t -> p c t i", i=4),
+            in_=q_raw[:].rearrange("p t (c i) -> p c t i", i=4),
+        )
+        q_codes = keep.tile([P, Q], U32, align_bytes=64, name="q_codes")
+        q_scales = keep.tile([P, Q], U8, align_bytes=64, name="q_scales")
+        nc.vector.quantize_mx(
+            out=q_codes[:].bitcast(FP8X4),
+            scales=q_scales[:],
+            in_=q_bf[:].rearrange("p q t -> p (q t)"),
+        )
+        base_sb = keep.tile([P, I], F32, name="base_sb", tag="rows")
+        nc.sync.dma_start(out=base_sb[:], in_=base)
+
+        a = keep.tile([P, T], F32, name="a")
+        for b in range(T // N_MM):
+            cols = slice(b * N_MM, (b + 1) * N_MM)
+            bank = psum.tile([P, N_MM], F32, name="bank%d" % b)
+            nc.tensor.matmul_mx(
+                out=bank[:],
+                lhsT=q_codes[:].bitcast(FP8X4),
+                lhsT_scale=q_scales[:],
+                rhs=k_words[:, 2 * b * N_MM : 2 * (b + 1) * N_MM].bitcast(FP4X4),
+                rhs_scale=k_scales[:, cols],
+                start=True,
+                stop=True,
+            )
+            if b % 2 == 0:
+                nc.scalar.activation(out=a[:, cols], in_=bank[:], func=ACT.Copy)
+            else:
+                nc.vector.tensor_copy(out=a[:, cols], in_=bank[:])
+
+        def wide(name, c):
+            return keep.tile([P, CHUNK], F32, name="%s%d" % (name, c))
+
+        def picked(n, c):
+            return a[:].indirect(lists[n][:, c * CHUNK // 16 : (c + 1) * CHUNK // 16])
+
+        half1 = [wide("half1", c) for c in range(CHUNKS)]
+        a2 = [wide("a2", c) for c in range(CHUNKS)]
+        a3 = [wide("a3", c) for c in range(CHUNKS)]
+        for c in range(CHUNKS):
+            nc.vector.tensor_scalar(half1[c][:], picked(0, c), 0.5, 0.0, ALU.mult, ALU.add)
+            nc.scalar.activation(a2[c][:], picked(1, c), ACT.Copy)
+            nc.scalar.activation(a3[c][:], picked(2, c), ACT.Copy)
+
+        mid = [wide("mid", c) for c in range(CHUNKS)]
+        gap = [wide("gap", c) for c in range(CHUNKS)]
+        off = [wide("off", c) for c in range(CHUNKS)]
+        gap_abs = [wide("gap_abs", c) for c in range(CHUNKS)]
+        off_abs = [wide("off_abs", c) for c in range(CHUNKS)]
+        for c in range(CHUNKS):
+            nc.vector.scalar_tensor_tensor(mid[c][:], a2[c][:], 0.5, half1[c][:], ALU.mult, ALU.add)
+            nc.vector.scalar_tensor_tensor(gap[c][:], a2[c][:], 0.5, half1[c][:], ALU.mult, ALU.subtract)
+            nc.vector.tensor_tensor(off[c][:], a3[c][:], mid[c][:], ALU.subtract)
+            nc.scalar.activation(gap_abs[c][:], gap[c][:], ACT.Abs)
+            nc.scalar.activation(off_abs[c][:], off[c][:], ACT.Abs)
+
+        part0 = [wide("part0", c) for c in range(CHUNKS)]
+        part1 = [wide("part1", c) for c in range(CHUNKS)]
+        reach = [wide("reach", c) for c in range(CHUNKS)]
+        neg_s = [wide("neg_s", c) for c in range(CHUNKS)]
+        neg_bm = keep.tile([P, G], F32, name="neg_bm")
+        neg_top = [keep.tile([P, 1], F32, name="neg_top%d" % c) for c in range(CHUNKS)]
+        u = [wide("u", c) for c in range(CHUNKS)]
+        for c in range(CHUNKS):
+            nc.vector.scalar_tensor_tensor(part0[c][:], gap_abs[c][:], lam_col[:], mid[c][:], ALU.mult, ALU.subtract)
+            nc.vector.tensor_tensor(reach[c][:], gap_abs[c][:], off_abs[c][:], ALU.max)
+            nc.vector.scalar_tensor_tensor(part1[c][:], off[c][:], -1.0 / 3.0, part0[c][:], ALU.mult, ALU.add)
+            nc.vector.scalar_tensor_tensor(neg_s[c][:], reach[c][:], lam_col[:], part1[c][:], ALU.mult, ALU.add)
+            nc.vector.tensor_reduce(
+                neg_bm[:, c * RUNS : (c + 1) * RUNS],
+                neg_s[c][:].rearrange("p (g j) -> p g j", j=RUN),
+                AX.X,
+                ALU.min,
+            )
+            nc.vector.tensor_reduce(neg_top[c][:], neg_bm[:, 0 : (c + 1) * RUNS], AX.X, ALU.min)
+            nc.scalar.activation(u[c][:], neg_s[c][:], ACT.Exp, bias=neg_top[c][:], scale=-1.0)
+
+        eg = keep.tile([P, G], F32, name="eg")
+        eg_sum = keep.tile([P, 1], F32, name="eg_sum")
+        nc.scalar.activation(eg[:], neg_bm[:], ACT.Exp, bias=neg_top[-1][:], scale=-1.0, accum_out=eg_sum[:])
+        inv_sum = keep.tile([P, 1], F32, name="inv_sum")
+        nc.vector.reciprocal(inv_sum[:], eg_sum[:])
+        factor = keep.tile([P, 1], F32, name="factor")
+        nc.vector.tensor_scalar(factor[:], inv_sum[:], gain_col[:], 128.0, ALU.mult, ALU.mult)
+
+        for c in range(CHUNKS):
+            run_sum = keep.tile([P, RUNS], F32, name="run_sum%d" % c)
+            nc.vector.tensor_reduce(run_sum[:], u[c][:].rearrange("p (g j) -> p g j", j=RUN), AX.X, ALU.add)
+            inv_run = keep.tile([P, RUNS], F32, name="inv_run%d" % c)
+            nc.vector.reciprocal(inv_run[:], run_sum[:])
+            share = keep.tile([P, RUNS], F32, name="share%d" % c)
+            nc.vector.scalar_tensor_tensor(
+                share[:], inv_run[:], BIG, eg[:, c * RUNS : (c + 1) * RUNS], ALU.min, ALU.mult
+            )
+            w = wide("w", c)
+            nc.vector.tensor_tensor(
+                w[:].rearrange("p (g j) -> p g j", j=RUN),
+                u[c][:].rearrange("p (g j) -> p g j", j=RUN),
+                share[:].unsqueeze(2).to_broadcast([P, RUNS, RUN]),
+                ALU.mult,
+            )
+            gated = wide("gated", c)
+            nc.scalar.activation(gated[:], w[:], ACT.Tanh, scale=factor[:])
+            y = wide("y", c)
+            nc.vector.tensor_tensor(y[:], gated[:], base_sb[:, c * CHUNK : (c + 1) * CHUNK], ALU.add)
+            nc.sync.dma_start(out=out[:, c * CHUNK : (c + 1) * CHUNK], in_=y[:])

@@ -19,7 +19,8 @@ AX = mybir.AxisListType
 
 P = 128
 RUN = I // G
-N_MM = 256
+PASS_WIDTHS = (512, 256, 128, 128)
+PIECES = ((0, 0, 256), (1, 0, 128), (1, 128, 128))
 CHUNK = 256
 CHUNKS = I // CHUNK
 RUNS = CHUNK // RUN
@@ -50,17 +51,13 @@ def tile_attend_spreadof3_bestofruns_gated_heads_kernel(
             tile = keep.tile([P, I // 16], U16, name="list%d" % n)
             nc.sync.dma_start(tile[:], src)
             lists.append(tile)
-        lam_col = keep.tile([P, 1], F32, name="lam_col")
-        nc.gpsimd.dma_start(out=lam_col[:], in_=lam)
-        gain_col = keep.tile([P, 1], F32, name="gain_col")
-        nc.gpsimd.dma_start(out=gain_col[:], in_=gain2)
 
-        q_bf = keep.tile([P, Q, 4], BF16, align_bytes=64, name="q_bf")
+        q_bf = keep.tile([P, Q, 4], BF16, align_bytes=64, name="q_bf", tag="cast")
         nc.vector.tensor_copy(
             out=q_bf[:].rearrange("p (c i) t -> p c t i", i=4),
             in_=q_raw[:].rearrange("p t (c i) -> p c t i", i=4),
         )
-        q_codes = keep.tile([P, Q], U32, align_bytes=64, name="q_codes")
+        q_codes = keep.tile([P, Q], U32, align_bytes=64, name="q_codes", tag="codes")
         q_scales = keep.tile([P, Q], U8, align_bytes=64, name="q_scales")
         nc.vector.quantize_mx(
             out=q_codes[:].bitcast(FP8X4),
@@ -69,24 +66,30 @@ def tile_attend_spreadof3_bestofruns_gated_heads_kernel(
         )
         base_sb = keep.tile([P, I], F32, name="base_sb", tag="rows")
         nc.sync.dma_start(out=base_sb[:], in_=base)
+        lam_col = keep.tile([P, 1], F32, align_bytes=64, name="lam_col", tag="cast")
+        nc.sync.dma_start(out=lam_col[:], in_=lam)
 
         a = keep.tile([P, T], F32, name="a")
-        for b in range(T // N_MM):
-            cols = slice(b * N_MM, (b + 1) * N_MM)
-            bank = psum.tile([P, N_MM], F32, name="bank%d" % b)
+        first = 0
+        for b, width in enumerate(PASS_WIDTHS):
+            cols = slice(first, first + width)
+            bank = psum.tile([P, width], F32, name="bank%d" % b)
             nc.tensor.matmul_mx(
                 out=bank[:],
                 lhsT=q_codes[:].bitcast(FP8X4),
                 lhsT_scale=q_scales[:],
-                rhs=k_words[:, 2 * b * N_MM : 2 * (b + 1) * N_MM].bitcast(FP4X4),
+                rhs=k_words[:, 2 * first : 2 * (first + width)].bitcast(FP4X4),
                 rhs_scale=k_scales[:, cols],
                 start=True,
                 stop=True,
             )
-            if b % 2 == 0:
+            if b in (0, 3):
                 nc.scalar.activation(out=a[:, cols], in_=bank[:], func=ACT.Copy)
             else:
                 nc.vector.tensor_copy(out=a[:, cols], in_=bank[:])
+            first = first + width
+        gain_col = keep.tile([P, 1], F32, align_bytes=64, name="gain_col", tag="codes")
+        nc.sync.dma_start(out=gain_col[:], in_=gain2)
 
         def wide(name, c):
             return keep.tile([P, CHUNK], F32, name="%s%d" % (name, c))
@@ -126,6 +129,7 @@ def tile_attend_spreadof3_bestofruns_gated_heads_kernel(
             nc.vector.tensor_tensor(reach[c][:], gap_abs[c][:], off_abs[c][:], ALU.max)
             nc.vector.scalar_tensor_tensor(part1[c][:], off[c][:], -1.0 / 3.0, part0[c][:], ALU.mult, ALU.add)
             nc.vector.scalar_tensor_tensor(neg_s[c][:], reach[c][:], lam_col[:], part1[c][:], ALU.mult, ALU.add)
+        for c in range(CHUNKS):
             nc.vector.tensor_reduce(
                 neg_bm[:, c * RUNS : (c + 1) * RUNS],
                 neg_s[c][:].rearrange("p (g j) -> p g j", j=RUN),
@@ -133,34 +137,45 @@ def tile_attend_spreadof3_bestofruns_gated_heads_kernel(
                 ALU.min,
             )
             nc.vector.tensor_reduce(neg_top[c][:], neg_bm[:, 0 : (c + 1) * RUNS], AX.X, ALU.min)
-            nc.scalar.activation(u[c][:], neg_s[c][:], ACT.Exp, bias=neg_top[c][:], scale=-1.0)
 
+        gain128 = keep.tile([P, 1], F32, name="gain128")
+        nc.scalar.activation(gain128[:], gain_col[:], ACT.Copy, scale=128.0)
         eg = keep.tile([P, G], F32, name="eg")
-        eg_sum = keep.tile([P, 1], F32, name="eg_sum")
-        nc.scalar.activation(eg[:], neg_bm[:], ACT.Exp, bias=neg_top[-1][:], scale=-1.0, accum_out=eg_sum[:])
-        inv_sum = keep.tile([P, 1], F32, name="inv_sum")
-        nc.vector.reciprocal(inv_sum[:], eg_sum[:])
-        factor = keep.tile([P, 1], F32, name="factor")
-        nc.vector.tensor_scalar(factor[:], inv_sum[:], gain_col[:], 128.0, ALU.mult, ALU.mult)
-
-        for c in range(CHUNKS):
-            run_sum = keep.tile([P, RUNS], F32, name="run_sum%d" % c)
-            nc.vector.tensor_reduce(run_sum[:], u[c][:].rearrange("p (g j) -> p g j", j=RUN), AX.X, ALU.add)
-            inv_run = keep.tile([P, RUNS], F32, name="inv_run%d" % c)
-            nc.vector.reciprocal(inv_run[:], run_sum[:])
-            share = keep.tile([P, RUNS], F32, name="share%d" % c)
-            nc.vector.scalar_tensor_tensor(
-                share[:], inv_run[:], BIG, eg[:, c * RUNS : (c + 1) * RUNS], ALU.min, ALU.mult
+        sums = [keep.tile([P, w // RUN + (n == 0)], F32, name="sums%d" % n) for n, (c, f, w) in enumerate(PIECES)]
+        for n, (c, f, w) in enumerate(PIECES):
+            nc.scalar.activation(
+                u[c][:, f : f + w], neg_s[c][:, f : f + w], ACT.Exp, bias=neg_top[c][:], scale=-1.0
             )
-            w = wide("w", c)
+            if n == 0:
+                nc.scalar.activation(
+                    eg[:], neg_bm[:], ACT.Exp, bias=neg_top[-1][:], scale=-1.0,
+                    accum_out=sums[0][:, w // RUN : w // RUN + 1],
+                )
+        factor = keep.tile([P, 1], F32, name="factor")
+        gated = []
+        for n, (c, f, w) in enumerate(PIECES):
+            runs = w // RUN
+            u_runs = u[c][:, f : f + w].rearrange("p (g j) -> p g j", j=RUN)
+            nc.vector.tensor_reduce(sums[n][:, 0:runs], u_runs, AX.X, ALU.add)
+            inv = keep.tile([P, runs + (n == 0)], F32, name="inv%d" % n)
+            nc.vector.reciprocal(inv[:], sums[n][:])
+            if n == 0:
+                nc.scalar.activation(factor[:], inv[:, runs : runs + 1], ACT.Copy, scale=gain128[:])
+            share = keep.tile([P, runs], F32, name="share%d" % n)
+            g0 = (c * CHUNK + f) // RUN
+            nc.vector.scalar_tensor_tensor(share[:], inv[:, 0:runs], BIG, eg[:, g0 : g0 + runs], ALU.min, ALU.mult)
+            weight = keep.tile([P, w], F32, name="weight%d" % n)
             nc.vector.tensor_tensor(
-                w[:].rearrange("p (g j) -> p g j", j=RUN),
-                u[c][:].rearrange("p (g j) -> p g j", j=RUN),
-                share[:].unsqueeze(2).to_broadcast([P, RUNS, RUN]),
+                weight[:].rearrange("p (g j) -> p g j", j=RUN),
+                u_runs,
+                share[:].unsqueeze(2).to_broadcast([P, runs, RUN]),
                 ALU.mult,
             )
-            gated = wide("gated", c)
-            nc.scalar.activation(gated[:], w[:], ACT.Tanh, scale=factor[:])
-            y = wide("y", c)
-            nc.vector.tensor_tensor(y[:], gated[:], base_sb[:, c * CHUNK : (c + 1) * CHUNK], ALU.add)
-            nc.sync.dma_start(out=out[:, c * CHUNK : (c + 1) * CHUNK], in_=y[:])
+            t = keep.tile([P, w], F32, name="gated%d" % n)
+            nc.scalar.activation(t[:], weight[:], ACT.Tanh, scale=factor[:])
+            gated.append(t)
+        for n, (c, f, w) in enumerate(PIECES):
+            cols = slice(c * CHUNK + f, c * CHUNK + f + w)
+            y = keep.tile([P, w], F32, name="y%d" % n)
+            nc.vector.tensor_tensor(y[:], gated[n][:], base_sb[:, cols], ALU.add)
+            nc.sync.dma_start(out=out[:, cols], in_=y[:])

@@ -101,8 +101,8 @@ def tile_attend_spreadof3_bestofruns_gated_heads_kernel(
         a2 = [wide("a2", c) for c in range(CHUNKS)]
         a3 = [wide("a3", c) for c in range(CHUNKS)]
         for c in range(CHUNKS):
-            nc.vector.tensor_scalar(half1[c][:], picked(0, c), 0.5, 0.0, ALU.mult, ALU.add)
-            nc.scalar.activation(a2[c][:], picked(1, c), ACT.Copy)
+            nc.vector.tensor_copy(a2[c][:], picked(1, c))
+            nc.scalar.activation(half1[c][:], picked(0, c), ACT.Copy, scale=0.5)
             nc.scalar.activation(a3[c][:], picked(2, c), ACT.Copy)
 
         mid = [wide("mid", c) for c in range(CHUNKS)]

from contextlib import ExitStack

import concourse.mybir as mybir

D, T, I, Q, G = 512, 1024, 512, 128, 64
FLOPS = 2 * D * T * Q

F32 = mybir.dt.float32
BF16 = mybir.dt.bfloat16
I32 = mybir.dt.int32
U32 = mybir.dt.uint32
U16 = mybir.dt.uint16
U8 = mybir.dt.uint8
FP8X4 = mybir.dt.float8_e4m3fn_x4
FP4X4 = mybir.dt.float4_e2m1fn_x4
ALU = mybir.AluOpType
ACT = mybir.ActivationFunctionType
AX = mybir.AxisListType

P = 128
RUN = I // G
PASS_WIDTHS = (512, 256, 128, 128)
PIECES = ((0, 0, 256), (1, 0, 128), (1, 128, 128))
CHUNK = 256
CHUNKS = I // CHUNK
RUNS = CHUNK // RUN
BIG = 1e30


def tile_attend_spreadof3_bestofruns_gated_heads_kernel(
    tc, query, keys_words, keys_scales, lam, base, gain2, offs, offs2, offs3, out
):
    nc = tc.nc
    with ExitStack() as ctx:
        keep = ctx.enter_context(tc.tile_pool(name="keep", bufs=1))
        psum = ctx.enter_context(tc.psum_pool(name="psum", bufs=1))

        k_scales = keep.tile([P, T], U8, align_bytes=64, name="k_scales")
        nc.vector.memset(k_scales[:].bitcast(I32), 0)

        q_raw = keep.tile([P, 4, Q], F32, name="q_raw", tag="rows")
        nc.sync.dma_start(out=q_raw[:], in_=query.rearrange("(p j) q -> p j q", j=4))
        k_words = keep.tile([P, 2 * T], U8, align_bytes=64, name="k_words")
        nc.sync.dma_start(out=k_words[:].bitcast(I32), in_=keys_words[0].bitcast(I32))
        for r in range(4):
            nc.scalar.dma_start(
                out=k_scales[r:P:32, :].bitcast(I32), in_=keys_scales[0][r:16:4, :].bitcast(I32)
            )
        lists = []
        for n, src in enumerate((offs, offs2, offs3)):
            tile = keep.tile([P, I // 16], U16, name="list%d" % n)
            nc.sync.dma_start(tile[:], src)
            lists.append(tile)

        q_bf = keep.tile([P, Q, 4], BF16, align_bytes=64, name="q_bf", tag="cast")
        nc.vector.tensor_copy(
            out=q_bf[:].rearrange("p (c i) t -> p c t i", i=4),
            in_=q_raw[:].rearrange("p t (c i) -> p c t i", i=4),
        )
        q_codes = keep.tile([P, Q], U32, align_bytes=64, name="q_codes", tag="codes")
        q_scales = keep.tile([P, Q], U8, align_bytes=64, name="q_scales")
        nc.vector.quantize_mx(
            out=q_codes[:].bitcast(FP8X4),
            scales=q_scales[:],
            in_=q_bf[:].rearrange("p q t -> p (q t)"),
        )
        base_sb = keep.tile([P, I], F32, name="base_sb", tag="rows")
        nc.sync.dma_start(out=base_sb[:], in_=base)
        lam_col = keep.tile([P, 1], F32, align_bytes=64, name="lam_col", tag="cast")
        nc.sync.dma_start(out=lam_col[:], in_=lam)

        a = keep.tile([P, T], F32, name="a")
        first = 0
        for b, width in enumerate(PASS_WIDTHS):
            cols = slice(first, first + width)
            bank = psum.tile([P, width], F32, name="bank%d" % b)
            nc.tensor.matmul_mx(
                out=bank[:],
                lhsT=q_codes[:].bitcast(FP8X4),
                lhsT_scale=q_scales[:],
                rhs=k_words[:, 2 * first : 2 * (first + width)].bitcast(FP4X4),
                rhs_scale=k_scales[:, cols],
                start=True,
                stop=True,
            )
            if b in (0, 3):
                nc.scalar.activation(out=a[:, cols], in_=bank[:], func=ACT.Copy)
            else:
                nc.vector.tensor_copy(out=a[:, cols], in_=bank[:])
            first = first + width
        gain_col = keep.tile([P, 1], F32, align_bytes=64, name="gain_col", tag="codes")
        nc.sync.dma_start(out=gain_col[:], in_=gain2)

        def wide(name, c):
            return keep.tile([P, CHUNK], F32, name="%s%d" % (name, c))

        def picked(n, c):
            return a[:].indirect(lists[n][:, c * CHUNK // 16 : (c + 1) * CHUNK // 16])

        half1 = [wide("half1", c) for c in range(CHUNKS)]
        a2 = [wide("a2", c) for c in range(CHUNKS)]
        a3 = [wide("a3", c) for c in range(CHUNKS)]
        for c in range(CHUNKS):
            nc.vector.tensor_copy(a2[c][:], picked(1, c))
            nc.scalar.activation(half1[c][:], picked(0, c), ACT.Copy, scale=0.5)
            nc.scalar.activation(a3[c][:], picked(2, c), ACT.Copy)

        mid = [wide("mid", c) for c in range(CHUNKS)]
        gap = [wide("gap", c) for c in range(CHUNKS)]
        off = [wide("off", c) for c in range(CHUNKS)]
        gap_abs = [wide("gap_abs", c) for c in range(CHUNKS)]
        off_abs = [wide("off_abs", c) for c in range(CHUNKS)]
        for c in range(CHUNKS):
            nc.vector.scalar_tensor_tensor(mid[c][:], a2[c][:], 0.5, half1[c][:], ALU.mult, ALU.add)
            nc.vector.scalar_tensor_tensor(gap[c][:], a2[c][:], 0.5, half1[c][:], ALU.mult, ALU.subtract)
            nc.vector.tensor_tensor(off[c][:], a3[c][:], mid[c][:], ALU.subtract)
            nc.scalar.activation(gap_abs[c][:], gap[c][:], ACT.Abs)
            nc.scalar.activation(off_abs[c][:], off[c][:], ACT.Abs)

        part0 = [wide("part0", c) for c in range(CHUNKS)]
        part1 = [wide("part1", c) for c in range(CHUNKS)]
        reach = [wide("reach", c) for c in range(CHUNKS)]
        neg_s = [wide("neg_s", c) for c in range(CHUNKS)]
        neg_bm = keep.tile([P, G], F32, name="neg_bm")
        neg_top = [keep.tile([P, 1], F32, name="neg_top%d" % c) for c in range(CHUNKS)]
        u = [wide("u", c) for c in range(CHUNKS)]
        for c in range(CHUNKS):
            nc.vector.scalar_tensor_tensor(part0[c][:], gap_abs[c][:], lam_col[:], mid[c][:], ALU.mult, ALU.subtract)
            nc.vector.tensor_tensor(reach[c][:], gap_abs[c][:], off_abs[c][:], ALU.max)
            nc.vector.scalar_tensor_tensor(part1[c][:], off[c][:], -1.0 / 3.0, part0[c][:], ALU.mult, ALU.add)
            nc.vector.scalar_tensor_tensor(neg_s[c][:], reach[c][:], lam_col[:], part1[c][:], ALU.mult, ALU.add)
        for c in range(CHUNKS):
            nc.vector.tensor_reduce(
                neg_bm[:, c * RUNS : (c + 1) * RUNS],
                neg_s[c][:].rearrange("p (g j) -> p g j", j=RUN),
                AX.X,
                ALU.min,
            )
            nc.vector.tensor_reduce(neg_top[c][:], neg_bm[:, 0 : (c + 1) * RUNS], AX.X, ALU.min)

        gain128 = keep.tile([P, 1], F32, name="gain128")
        nc.scalar.activation(gain128[:], gain_col[:], ACT.Copy, scale=128.0)
        eg = keep.tile([P, G], F32, name="eg")
        sums = [keep.tile([P, w // RUN + (n == 0)], F32, name="sums%d" % n) for n, (c, f, w) in enumerate(PIECES)]
        for n, (c, f, w) in enumerate(PIECES):
            nc.scalar.activation(
                u[c][:, f : f + w], neg_s[c][:, f : f + w], ACT.Exp, bias=neg_top[c][:], scale=-1.0
            )
            if n == 0:
                nc.scalar.activation(
                    eg[:], neg_bm[:], ACT.Exp, bias=neg_top[-1][:], scale=-1.0,
                    accum_out=sums[0][:, w // RUN : w // RUN + 1],
                )
        factor = keep.tile([P, 1], F32, name="factor")
        gated = []
        for n, (c, f, w) in enumerate(PIECES):
            runs = w // RUN
            u_runs = u[c][:, f : f + w].rearrange("p (g j) -> p g j", j=RUN)
            nc.vector.tensor_reduce(sums[n][:, 0:runs], u_runs, AX.X, ALU.add)
            inv = keep.tile([P, runs + (n == 0)], F32, name="inv%d" % n)
            nc.vector.reciprocal(inv[:], sums[n][:])
            if n == 0:
                nc.scalar.activation(factor[:], inv[:, runs : runs + 1], ACT.Copy, scale=gain128[:])
            share = keep.tile([P, runs], F32, name="share%d" % n)
            g0 = (c * CHUNK + f) // RUN
            nc.vector.scalar_tensor_tensor(share[:], inv[:, 0:runs], BIG, eg[:, g0 : g0 + runs], ALU.min, ALU.mult)
            weight = keep.tile([P, w], F32, name="weight%d" % n)
            nc.vector.tensor_tensor(
                weight[:].rearrange("p (g j) -> p g j", j=RUN),
                u_runs,
                share[:].unsqueeze(2).to_broadcast([P, runs, RUN]),
                ALU.mult,
            )
            t = keep.tile([P, w], F32, name="gated%d" % n)
            nc.scalar.activation(t[:], weight[:], ACT.Tanh, scale=factor[:])
            gated.append(t)
        for n, (c, f, w) in enumerate(PIECES):
            cols = slice(c * CHUNK + f, c * CHUNK + f + w)
            y = keep.tile([P, w], F32, name="y%d" % n)
            nc.vector.tensor_tensor(y[:], gated[n][:], base_sb[:, cols], ALU.add)
            nc.sync.dma_start(out=out[:, cols], in_=y[:])
